import numpy as np
import ml_dtypes


def mxq(x, axis, fmt="e4m3"):
    dtype, down = {"e4m3": (ml_dtypes.float8_e4m3fn, 7), "e5m2": (ml_dtypes.float8_e5m2, 14)}[fmt]
    v = np.moveaxis(np.asarray(x, np.float32).astype(ml_dtypes.bfloat16).astype(np.float64), axis, -1)
    blocks = v.reshape(v.shape[:-1] + (-1, 32))
    amax = np.abs(blocks).max(-1, keepdims=True)
    byte = np.maximum(np.where(amax > 0, np.frexp(amax)[1] - 1 + 127, 0) - down, 1)
    scale = np.exp2(byte - 127.0)
    codes = (blocks / scale).astype(np.float32).astype(dtype).astype(np.float64)
    return np.moveaxis((codes * scale).reshape(v.shape), -1, axis)


WIDE = False


def mx_kscale(k):
    if not WIDE:
        return np.ones(k)
    levels = np.array([10, -10, 5, -5, 0])
    if k % 512:
        return np.exp2(np.random.permutation(np.resize(levels, k // 32))).repeat(32)
    a = np.empty((k // 512, 16))
    for p in range(k // 512):
        a[p, :8] = np.random.permutation(np.resize(levels, 8))
        for g in range(8):
            far = levels[np.abs(levels - a[p, g]) >= 10]
            a[p, g + 8] = far[np.random.randint(len(far))]
    return np.exp2(a.ravel()).repeat(32)


def f64(x):
    return np.asarray(x).astype(np.float64)


def striped8(idx):
    return np.asarray(idx).reshape(8, -1, 16).transpose(0, 2, 1).reshape(128, -1).astype(np.uint16)


def unstriped8(offs):
    return offs.reshape(8, 16, -1).transpose(0, 2, 1).reshape(8, -1).astype(np.int64)


def pick8(x, idx, run):
    r = np.arange(len(x))
    return x[r[:, None], idx[r % (8 * run) // run]]


E2M1 = np.array([0.0, 0.5, 1.0, 1.5, 2.0, 3.0, 4.0, 6.0, -0.0, -0.5, -1.0, -1.5, -2.0, -3.0, -4.0, -6.0])


def pack_weight(w, fmt):
    k, n = w.shape
    w = f64(np.asarray(w, np.float32).astype(ml_dtypes.bfloat16)).reshape(k // 32, 32, n)
    amax = np.abs(w).max(1)
    if fmt == "e4m3":
        byte = np.frexp(amax)[1] - 1 + 127 - 7
    else:
        mant, ex = np.frexp(amax / 6.0)
        byte = np.where(mant > 0.5, ex, ex - 1) + 127
    byte = np.clip(np.where(amax > 0, byte, 1), 1, 254)
    scaled = (w * np.exp2(127.0 - byte)[:, None, :]).reshape(k, n).astype(np.float32)
    by_word = np.ascontiguousarray(scaled.reshape(k // 512, 128, 4, n).transpose(0, 1, 3, 2))
    if fmt == "e4m3":
        words = by_word.astype(ml_dtypes.float8_e4m3fn).view(np.uint8)
    else:
        c = by_word.astype(ml_dtypes.float4_e2m1fn).view(np.uint8) & 0xF
        words = (c[..., 0::2] | (c[..., 1::2] << 4)).reshape(k // 512, 128, 2 * n)
    return np.ascontiguousarray(words), np.ascontiguousarray(byte.astype(np.uint8).reshape(k // 512, 16, n))


def unpack_weight(words, scales, fmt):
    g, _, n = scales.shape
    words = np.ascontiguousarray(words).reshape(g, 128, n, -1)
    if fmt == "e4m3":
        vals = words.view(ml_dtypes.float8_e4m3fn).astype(np.float64)
    else:
        nib = np.empty((g, 128, n, 4), np.uint8)
        nib[..., 0::2] = words & 0xF
        nib[..., 1::2] = words >> 4
        vals = E2M1[nib]
    vals = vals * np.repeat(np.exp2(scales.astype(np.float64) - 127.0), 8, axis=1)[..., None]
    return vals.transpose(0, 1, 3, 2).reshape(g * 512, n)


def sigmoid(v):
    return 1.0 / (1.0 + np.exp(-v))


D, E, T, Q, I = 512, 512, 1024, 128, 512


def setup_inputs():
    n = np.random.standard_normal
    idx = np.stack([np.random.permutation(T)[:I] for _ in range(8)])
    fd = mx_kscale(D)
    fe = mx_kscale(E)
    keysp = pack_weight(n((D, T)) / fd[:, None], "e4m3")
    return {
        "query": (n((D, Q)) * 0.4 / np.sqrt(D) * fd[:, None]).astype(np.float32),
        "keys_words": keysp[0],
        "keys_scales": keysp[1],
        "gout": (n((E, Q)) * 1 / np.sqrt(E) * fe[:, None]).astype(np.float32),
        "vals": (n((E, T)) / fe[:, None]).astype(np.float32),
        "steep": (np.random.uniform(2.0, 5.0, (Q, 1))).astype(np.float32),
        "boost": (np.random.uniform(0.5, 2.0, (1, I))).astype(np.float32),
        "fac": (np.random.uniform(0.5, 2.0, (1, T))).astype(np.float32),
        "old": (0.5 * n((Q, T))).astype(np.float32),
        "offs": striped8(idx),
    }


def reference(query, keys_words, keys_scales, gout, vals, steep, boost, fac, old, offs):
    idx = unstriped8(offs)
    keysu = unpack_weight(keys_words, keys_scales, "e4m3")
    queryq = mxq(f64(query), 0, "e4m3")
    a = queryq.T @ keysu
    b = sigmoid(pick8(a, idx, 16) * f64(steep))
    bb = b * f64(boost)
    bf = np.zeros((Q, T))
    bf[np.arange(Q)[:, None], idx[np.arange(Q) % 128 // 16]] = bb
    s = a + bf
    p = np.exp(s - np.max(s, axis=1, keepdims=True))
    z = np.sum(p, axis=1, keepdims=True)
    goutq = mxq(f64(gout), 0, "e4m3")
    valsq = mxq(f64(vals), 0, "e4m3")
    c0 = goutq.T @ valsq
    dz = np.sum(c0 * p * f64(fac) / np.square(z) * (-1.0), axis=1, keepdims=True)
    dp = c0 / z * f64(fac) + dz
    ds = dp * p
    dbb = pick8(ds, idx, 16)
    db = dbb * f64(boost)
    e1 = db * b * (1.0 - b) * f64(steep)
    s1 = np.zeros((Q, T))
    s1[np.arange(Q)[:, None], idx[np.arange(Q) % 128 // 16]] = e1
    da = ds + s1
    y = da * 1024.0 + f64(old)
    return y

@@ -1,0 +1,218 @@
+from contextlib import ExitStack
+
+import concourse.mybir as mybir
+from concourse.masks import make_identity
+
+F32 = mybir.dt.float32
+BF16 = mybir.dt.bfloat16
+I32 = mybir.dt.int32
+U32 = mybir.dt.uint32
+U16 = mybir.dt.uint16
+U8 = mybir.dt.uint8
+FP8X4 = mybir.dt.float8_e4m3fn_x4
+ALU = mybir.AluOpType
+ACT = mybir.ActivationFunctionType
+
+P = 128
+PACK = 4
+T = 1024
+SLOTS = 512
+BANK = 512
+CHUNK = 256
+OUT_SCALE = 1024.0
+
+FLOPS = 2 * 2 * 512 * P * T
+
+
+def interleave(engine_copy, grouped, raw):
+    engine_copy(
+        grouped.rearrange("p (c i) j -> p c j i", i=4),
+        raw.rearrange("p j (c i) -> p c j i", i=4),
+    )
+
+
+def tile_attend_bboost_heads_kernel(tc, query, keys_words, keys_scales, gout, vals, steep, boost, fac, old, offs, out):
+    nc = tc.nc
+    halves = [slice(h * BANK, (h + 1) * BANK) for h in range(T // BANK)]
+    blocks = [slice(c * P, (c + 1) * P) for c in range(T // P)]
+    chunks = [slice(c * CHUNK, (c + 1) * CHUNK) for c in range(T // CHUNK)]
+
+    with ExitStack() as ctx:
+        sb = ctx.enter_context(tc.tile_pool(name="sb", bufs=1))
+        ps = ctx.enter_context(tc.psum_pool(name="ps", bufs=1))
+
+        offsets = sb.tile([P, SLOTS // 16], U16, name="offsets")
+        key_scales = sb.tile([P, T], U8, name="key_scales", align_bytes=64)
+        nc.vector.memset(key_scales[:].bitcast(I32), 0)
+
+        steep_col = sb.tile([P, 1], F32, name="steep_col")
+        nc.gpsimd.dma_start(steep_col[:], steep)
+        q_raw = sb.tile([P, PACK, P], F32, name="q_raw")
+        nc.sync.dma_start(q_raw[:], query.rearrange("(p j) q -> p j q", j=PACK))
+        nc.sync.dma_start(offsets[:], offs)
+        for quad in range(4):
+            nc.sync.dma_start(
+                key_scales[32 * quad : 32 * quad + 4, :].bitcast(I32),
+                keys_scales[0, 4 * quad : 4 * quad + 4, :].bitcast(I32),
+            )
+        key_words = [sb.tile([P, BANK], U32, name=f"key_words{h}", align_bytes=64) for h in range(2)]
+        words_in = keys_words[0].rearrange("p n t -> p (n t)").bitcast(I32)
+        for h in range(2):
+            nc.sync.dma_start(key_words[h][:].bitcast(I32), words_in[:, halves[h]])
+        boost_cols = sb.tile([P, 4], F32, name="boost_cols")
+        nc.sync.dma_start(boost_cols[:], boost[0].rearrange("(n j) -> n j", j=4))
+        v_raw = [sb.tile([P, PACK, CHUNK], F32, name=f"v_raw{c}") for c in range(len(chunks))]
+        vals_rows = vals.rearrange("(p j) t -> p j t", j=PACK)
+        g_raw = sb.tile([P, PACK, P], F32, name="g_raw")
+        nc.sync.dma_start(g_raw[:], gout.rearrange("(p j) q -> p j q", j=PACK))
+        for c in range(len(chunks)):
+            nc.sync.dma_start(v_raw[c][:], vals_rows[:, :, chunks[c]])
+        fac_row = sb.tile([P, T], F32, name="fac_row")
+        nc.sync.dma_start(fac_row[:], fac[0].partition_broadcast(P))
+        old_sb = sb.tile([P, T], F32, name="old_sb")
+        nc.sync.dma_start(old_sb[:], old)
+
+        ident = sb.tile([P, P], F32, name="ident")
+        make_identity(nc, ident[:])
+        bf = sb.tile([P, T], F32, name="bf")
+        nc.vector.memset(bf[:].bitcast(I32), 0)
+        s1 = sb.tile([P, T], F32, name="s1")
+        nc.vector.memset(s1[:].bitcast(I32), 0)
+
+        q_bf = sb.tile([P, P, PACK], BF16, name="q_bf", align_bytes=64)
+        interleave(nc.vector.tensor_copy, q_bf[:], q_raw[:])
+        q_codes = sb.tile([P, P], U32, name="q_codes", align_bytes=64)
+        q_scales = sb.tile([P, P], U8, name="q_scales", align_bytes=64)
+        nc.vector.quantize_mx(q_codes[:].bitcast(FP8X4), q_scales[:], q_bf[:].rearrange("p q j -> p (q j)"))
+        a_cuts = [(0, 512), (512, 768), (768, 1024)]
+        a_ps = [ps.tile([P, hi - lo], F32, name=f"a_ps{n}", tag=f"a_ps{n}") for n, (lo, hi) in enumerate(a_cuts)]
+        for n, (lo, hi) in enumerate(a_cuts):
+            h = lo // BANK
+            nc.tensor.matmul_mx(
+                a_ps[n][:],
+                lhsT=q_codes[:].bitcast(FP8X4),
+                lhsT_scale=q_scales[:],
+                rhs=key_words[h][:, lo - h * BANK : hi - h * BANK].bitcast(FP8X4),
+                rhs_scale=key_scales[:, lo:hi],
+                start=True,
+                stop=True,
+            )
+
+        neg_half = sb.tile([P, 1], F32, name="neg_half")
+        nc.gpsimd.memset(neg_half[:], -0.5)
+        quarter_steep = sb.tile([P, 1], F32, name="quarter_steep")
+        nc.gpsimd.tensor_scalar(quarter_steep[:], steep_col[:], 0.25, 0.0, ALU.mult, ALU.add)
+        neg_steep = sb.tile([P, 1], F32, name="neg_steep")
+        nc.gpsimd.tensor_scalar(neg_steep[:], steep_col[:], -1.0, 0.0, ALU.mult, ALU.add)
+
+        a_sb = sb.tile([P, T], F32, name="a_sb")
+        nc.scalar.copy(a_sb[:, halves[0]], a_ps[0][:])
+        for n in (1, 2):
+            nc.vector.tensor_copy(a_sb[:, a_cuts[n][0] : a_cuts[n][1]], a_ps[n][:])
+
+        boost_ps = ps.tile([P, 4, P], F32, name="boost_ps", tag="a_ps0")
+        for j in range(4):
+            nc.tensor.transpose(boost_ps[:, j, :], boost_cols[:, j : j + 1].to_broadcast([P, P]), ident[:])
+
+        slot_halves = [slice(h * SLOTS // 2, (h + 1) * SLOTS // 2) for h in range(2)]
+        b_sig = sb.tile([P, SLOTS], F32, name="b_sig")
+        for h in range(2):
+            a_listed = sb.tile([P, SLOTS // 2], F32, name=f"a_listed{h}", tag=f"a_listed{h}", align_bytes=64)
+            nc.vector.tensor_copy(a_listed[:], a_sb[:].indirect(offsets[:, 16 * h : 16 * (h + 1)]))
+            nc.scalar.activation(b_sig[:, slot_halves[h]], a_listed[:], ACT.Sigmoid, scale=steep_col[:])
+        boost_row = sb.tile([P, SLOTS], F32, name="boost_row")
+        nc.vector.tensor_copy(boost_row[:].rearrange("p (n j) -> p n j", j=4), boost_ps[:].rearrange("p j n -> p n j"))
+
+        g_bf = sb.tile([P, P, PACK], BF16, name="g_bf", align_bytes=64)
+        g_codes = sb.tile([P, P], U32, name="g_codes", align_bytes=64)
+        g_scales = sb.tile([P, P], U8, name="g_scales", align_bytes=64)
+        v_bf = [sb.tile([P, CHUNK, PACK], BF16, name=f"v_bf{c}", tag=("a_listed1" if c == 0 else f"v_bf{c}"), align_bytes=64) for c in range(len(chunks))]
+        v_codes = sb.tile([P, T], U32, name="v_codes", align_bytes=64)
+        v_scales = sb.tile([P, T], U8, name="v_scales", align_bytes=64)
+
+        def quantise_vals(c):
+            nc.vector.quantize_mx(
+                v_codes[:, chunks[c]].bitcast(FP8X4), v_scales[:, chunks[c]], v_bf[c][:].rearrange("p t j -> p (t j)")
+            )
+
+        interleave(nc.scalar.copy, g_bf[:], g_raw[:])
+        nc.vector.quantize_mx(g_codes[:].bitcast(FP8X4), g_scales[:], g_bf[:].rearrange("p q j -> p (q j)"))
+        for c in range(len(chunks)):
+            interleave(nc.scalar.copy, v_bf[c][:], v_raw[c][:])
+
+        nc.vector.tensor_tensor(bf[:].indirect(offsets[:]), b_sig[:], boost_row[:], ALU.mult)
+
+        quantise_vals(0)
+        quantise_vals(1)
+        s = sb.tile([P, T], F32, name="s", tag="v_bf1", align_bytes=64)
+        nc.vector.tensor_tensor(s[:], a_sb[:], bf[:], ALU.add)
+        quantise_vals(2)
+        neg_max = sb.tile([P, 1], F32, name="neg_max")
+        nc.vector.tensor_reduce(neg_max[:], s[:], mybir.AxisListType.X, ALU.max, negate=True)
+        quantise_vals(3)
+
+        c0_ps = [ps.tile([P, BANK], F32, name=f"c0_ps{h}", tag=f"c0_ps{h}") for h in range(2)]
+        for h in range(2):
+            nc.tensor.matmul_mx(
+                c0_ps[h][:],
+                lhsT=g_codes[:].bitcast(FP8X4),
+                lhsT_scale=g_scales[:],
+                rhs=v_codes[:, halves[h]].bitcast(FP8X4),
+                rhs_scale=v_scales[:, halves[h]],
+                start=True,
+                stop=True,
+            )
+
+        p = sb.tile([P, T], F32, name="p")
+        z = sb.tile([P, 1], F32, name="z")
+        nc.scalar.activation(p[:], s[:], ACT.Exp, bias=neg_max[:], accum_out=z[:])
+        neg_u = sb.tile([P, T], F32, name="neg_u")
+        for h in range(2):
+            nc.vector.scalar_tensor_tensor(
+                neg_u[:, halves[h]], c0_ps[h][:], -1.0, fac_row[:, halves[h]], ALU.mult, ALU.mult
+            )
+        inv_z = sb.tile([P, 1], F32, name="inv_z", tag="inv_z")
+        nc.vector.reciprocal(inv_z[:], z[:])
+        pn = sb.tile([P, T], F32, name="pn")
+        nc.scalar.activation(pn[:], p[:], ACT.Copy, scale=inv_z[:])
+        neg_w = sb.tile([P, T], F32, name="neg_w")
+        neg_c = sb.tile([P, 1], F32, name="neg_c")
+        nc.vector.scalar_tensor_tensor(neg_w[:], neg_u[:], inv_z[:], p[:], ALU.mult, ALU.mult, accum_out=neg_c[:])
+        b_sq = sb.tile([P, SLOTS], F32, name="b_sq", tag="inv_z")
+        nc.scalar.activation(b_sq[:], b_sig[:], ACT.Square, bias=neg_half[:])
+        slope = sb.tile([P, SLOTS], F32, name="slope")
+        nc.scalar.activation(slope[:], b_sq[:], ACT.Identity, bias=quarter_steep[:], scale=neg_steep[:])
+        old_t = sb.tile([P, T], F32, name="old_t", tag="inv_z")
+        base_ps = [ps.tile([P, BANK], F32, name=f"base_ps{h}") for h in range(2)]
+        for h in range(2):
+            old_ps = ps.tile([P, 4, P], F32, name=f"old_ps{h}", tag=f"c0_ps{h}")
+            for j in range(4):
+                nc.tensor.transpose(old_ps[:, j, :], old_sb[:, blocks[4 * h + j]], ident[:])
+            nc.scalar.copy(old_t[:, halves[h]], old_ps[:].rearrange("p j n -> p (j n)"))
+        for h in range(2):
+            for j in range(4):
+                nc.tensor.matmul(
+                    base_ps[h][:, blocks[j]], old_t[:, blocks[4 * h + j]], ident[:], start=(j == 0), stop=False, is_transpose=True
+                )
+        ds = sb.tile([P, T], F32, name="ds")
+        nc.vector.scalar_tensor_tensor(ds[:], pn[:], neg_c[:], neg_w[:], ALU.mult, ALU.subtract)
+
+        db = sb.tile([P, SLOTS], F32, name="db")
+        nc.vector.tensor_tensor(db[:], ds[:].indirect(offsets[:]), boost_row[:], ALU.mult)
+        ds_t = sb.tile([P, T], F32, name="ds_t")
+        for h in range(2):
+            ds_ps = ps.tile([P, BANK], F32, name=f"ds_ps{h}", tag=f"a_ps{h}")
+            for j in range(4):
+                nc.tensor.transpose(ds_ps[:, blocks[j]], ds[:, blocks[4 * h + j]], ident[:])
+            nc.scalar.activation(ds_t[:, halves[h]], ds_ps[:], ACT.Copy, scale=OUT_SCALE)
+        for h in range(2):
+            for j in range(4):
+                nc.tensor.matmul(
+                    base_ps[h][:, blocks[j]], ds_t[:, blocks[4 * h + j]], ident[:], start=False, stop=(j == 3), is_transpose=True
+                )
+        nc.vector.tensor_tensor(s1[:].indirect(offsets[:]), db[:], slope[:], ALU.mult)
+
+        for h in range(2):
+            res = sb.tile([P, BANK], F32, name=f"res{h}")
+            nc.vector.scalar_tensor_tensor(res[:], s1[:, halves[h]], OUT_SCALE, base_ps[h][:], ALU.mult, ALU.add)
+            nc.sync.dma_start(out[:, halves[h]], res[:])

@@ -44,6 +44,10 @@ def tile_attend_bboost_heads_kernel(tc, query, keys_words, keys_scales, gout, va
         offsets = sb.tile([P, SLOTS // 16], U16, name="offsets")
         key_scales = sb.tile([P, T], U8, name="key_scales", align_bytes=64)
         nc.vector.memset(key_scales[:].bitcast(I32), 0)
+        warm = sb.tile([P, 1], F32, name="warm")
+        nc.vector.memset(warm[:], 0.0)
+        warm_out = sb.tile([P, 1], F32, name="warm_out")
+        nc.scalar.activation(warm_out[:], warm[:], ACT.Sigmoid)
 
         steep_col = sb.tile([P, 1], F32, name="steep_col")
         nc.gpsimd.dma_start(steep_col[:], steep)
@@ -76,10 +80,8 @@ def tile_attend_bboost_heads_kernel(tc, query, keys_words, keys_scales, gout, va
         make_identity(nc, ident[:])
         bf = sb.tile([P, T], F32, name="bf")
         nc.vector.memset(bf[:].bitcast(I32), 0)
-        s1 = sb.tile([P, T], F32, name="s1")
-        nc.vector.memset(s1[:].bitcast(I32), 0)
 
-        q_bf = sb.tile([P, P, PACK], BF16, name="q_bf", align_bytes=64)
+        q_bf = sb.tile([P, P, PACK], BF16, name="q_bf", tag="q_bf", align_bytes=64)
         interleave(nc.vector.tensor_copy, q_bf[:], q_raw[:])
         q_codes = sb.tile([P, P], U32, name="q_codes", align_bytes=64)
         q_scales = sb.tile([P, P], U8, name="q_scales", align_bytes=64)
@@ -98,6 +100,8 @@ def tile_attend_bboost_heads_kernel(tc, query, keys_words, keys_scales, gout, va
                 stop=True,
             )
 
+        s1 = sb.tile([P, T], F32, name="s1", tag="q_bf", align_bytes=64)
+        nc.vector.memset(s1[:].bitcast(I32), 0)
         neg_half = sb.tile([P, 1], F32, name="neg_half")
         nc.gpsimd.memset(neg_half[:], -0.5)
         quarter_steep = sb.tile([P, 1], F32, name="quarter_steep")
@@ -212,7 +216,9 @@ def tile_attend_bboost_heads_kernel(tc, query, keys_words, keys_scales, gout, va
                 )
         nc.vector.tensor_tensor(s1[:].indirect(offsets[:]), db[:], slope[:], ALU.mult)
 
-        for h in range(2):
-            res = sb.tile([P, BANK], F32, name=f"res{h}")
-            nc.vector.scalar_tensor_tensor(res[:], s1[:, halves[h]], OUT_SCALE, base_ps[h][:], ALU.mult, ALU.add)
-            nc.sync.dma_start(out[:, halves[h]], res[:])
+        for c in range(len(chunks)):
+            res = sb.tile([P, CHUNK], F32, name=f"res{c}")
+            nc.vector.scalar_tensor_tensor(
+                res[:], s1[:, chunks[c]], OUT_SCALE, base_ps[c // 2][:, chunks[c % 2]], ALU.mult, ALU.add
+            )
+            nc.sync.dma_start(out[:, chunks[c]], res[:])

from contextlib import ExitStack

import concourse.mybir as mybir
from concourse.masks import make_identity

F32 = mybir.dt.float32
BF16 = mybir.dt.bfloat16
I32 = mybir.dt.int32
U32 = mybir.dt.uint32
U16 = mybir.dt.uint16
U8 = mybir.dt.uint8
FP8X4 = mybir.dt.float8_e4m3fn_x4
ALU = mybir.AluOpType
ACT = mybir.ActivationFunctionType

P = 128
PACK = 4
T = 1024
SLOTS = 512
BANK = 512
CHUNK = 256
OUT_SCALE = 1024.0

FLOPS = 2 * 2 * 512 * P * T


def interleave(engine_copy, grouped, raw):
    engine_copy(
        grouped.rearrange("p (c i) j -> p c j i", i=4),
        raw.rearrange("p j (c i) -> p c j i", i=4),
    )


def tile_attend_bboost_heads_kernel(tc, query, keys_words, keys_scales, gout, vals, steep, boost, fac, old, offs, out):
    nc = tc.nc
    halves = [slice(h * BANK, (h + 1) * BANK) for h in range(T // BANK)]
    blocks = [slice(c * P, (c + 1) * P) for c in range(T // P)]
    chunks = [slice(c * CHUNK, (c + 1) * CHUNK) for c in range(T // CHUNK)]

    with ExitStack() as ctx:
        sb = ctx.enter_context(tc.tile_pool(name="sb", bufs=1))
        ps = ctx.enter_context(tc.psum_pool(name="ps", bufs=1))

        offsets = sb.tile([P, SLOTS // 16], U16, name="offsets")
        key_scales = sb.tile([P, T], U8, name="key_scales", align_bytes=64)
        nc.vector.memset(key_scales[:].bitcast(I32), 0)
        warm = sb.tile([P, 1], F32, name="warm")
        nc.vector.memset(warm[:], 0.0)
        warm_out = sb.tile([P, 1], F32, name="warm_out")
        nc.scalar.activation(warm_out[:], warm[:], ACT.Sigmoid)

        steep_col = sb.tile([P, 1], F32, name="steep_col")
        nc.gpsimd.dma_start(steep_col[:], steep)
        q_raw = sb.tile([P, PACK, P], F32, name="q_raw")
        nc.sync.dma_start(q_raw[:], query.rearrange("(p j) q -> p j q", j=PACK))
        nc.sync.dma_start(offsets[:], offs)
        for quad in range(4):
            nc.sync.dma_start(
                key_scales[32 * quad : 32 * quad + 4, :].bitcast(I32),
                keys_scales[0, 4 * quad : 4 * quad + 4, :].bitcast(I32),
            )
        key_words = [sb.tile([P, BANK], U32, name=f"key_words{h}", align_bytes=64) for h in range(2)]
        words_in = keys_words[0].rearrange("p n t -> p (n t)").bitcast(I32)
        for h in range(2):
            nc.sync.dma_start(key_words[h][:].bitcast(I32), words_in[:, halves[h]])
        boost_cols = sb.tile([P, 4], F32, name="boost_cols")
        nc.sync.dma_start(boost_cols[:], boost[0].rearrange("(n j) -> n j", j=4))
        v_raw = [sb.tile([P, PACK, CHUNK], F32, name=f"v_raw{c}") for c in range(len(chunks))]
        vals_rows = vals.rearrange("(p j) t -> p j t", j=PACK)
        g_raw = sb.tile([P, PACK, P], F32, name="g_raw")
        nc.sync.dma_start(g_raw[:], gout.rearrange("(p j) q -> p j q", j=PACK))
        for c in range(len(chunks)):
            nc.sync.dma_start(v_raw[c][:], vals_rows[:, :, chunks[c]])
        fac_row = sb.tile([P, T], F32, name="fac_row")
        nc.sync.dma_start(fac_row[:], fac[0].partition_broadcast(P))
        old_sb = sb.tile([P, T], F32, name="old_sb")
        nc.sync.dma_start(old_sb[:], old)

        ident = sb.tile([P, P], F32, name="ident")
        make_identity(nc, ident[:])
        bf = sb.tile([P, T], F32, name="bf")
        nc.vector.memset(bf[:].bitcast(I32), 0)

        q_bf = sb.tile([P, P, PACK], BF16, name="q_bf", tag="q_bf", align_bytes=64)
        interleave(nc.vector.tensor_copy, q_bf[:], q_raw[:])
        q_codes = sb.tile([P, P], U32, name="q_codes", align_bytes=64)
        q_scales = sb.tile([P, P], U8, name="q_scales", align_bytes=64)
        nc.vector.quantize_mx(q_codes[:].bitcast(FP8X4), q_scales[:], q_bf[:].rearrange("p q j -> p (q j)"))
        a_cuts = [(0, 512), (512, 768), (768, 1024)]
        a_ps = [ps.tile([P, hi - lo], F32, name=f"a_ps{n}", tag=f"a_ps{n}") for n, (lo, hi) in enumerate(a_cuts)]
        for n, (lo, hi) in enumerate(a_cuts):
            h = lo // BANK
            nc.tensor.matmul_mx(
                a_ps[n][:],
                lhsT=q_codes[:].bitcast(FP8X4),
                lhsT_scale=q_scales[:],
                rhs=key_words[h][:, lo - h * BANK : hi - h * BANK].bitcast(FP8X4),
                rhs_scale=key_scales[:, lo:hi],
                start=True,
                stop=True,
            )

        s1 = sb.tile([P, T], F32, name="s1", tag="q_bf", align_bytes=64)
        nc.vector.memset(s1[:].bitcast(I32), 0)
        neg_half = sb.tile([P, 1], F32, name="neg_half")
        nc.gpsimd.memset(neg_half[:], -0.5)
        quarter_steep = sb.tile([P, 1], F32, name="quarter_steep")
        nc.gpsimd.tensor_scalar(quarter_steep[:], steep_col[:], 0.25, 0.0, ALU.mult, ALU.add)
        neg_steep = sb.tile([P, 1], F32, name="neg_steep")
        nc.gpsimd.tensor_scalar(neg_steep[:], steep_col[:], -1.0, 0.0, ALU.mult, ALU.add)

        a_sb = sb.tile([P, T], F32, name="a_sb")
        nc.scalar.copy(a_sb[:, halves[0]], a_ps[0][:])
        for n in (1, 2):
            nc.vector.tensor_copy(a_sb[:, a_cuts[n][0] : a_cuts[n][1]], a_ps[n][:])

        boost_ps = ps.tile([P, 4, P], F32, name="boost_ps", tag="a_ps0")
        for j in range(4):
            nc.tensor.transpose(boost_ps[:, j, :], boost_cols[:, j : j + 1].to_broadcast([P, P]), ident[:])

        slot_halves = [slice(h * SLOTS // 2, (h + 1) * SLOTS // 2) for h in range(2)]
        b_sig = sb.tile([P, SLOTS], F32, name="b_sig")
        for h in range(2):
            a_listed = sb.tile([P, SLOTS // 2], F32, name=f"a_listed{h}", tag=f"a_listed{h}", align_bytes=64)
            nc.vector.tensor_copy(a_listed[:], a_sb[:].indirect(offsets[:, 16 * h : 16 * (h + 1)]))
            nc.scalar.activation(b_sig[:, slot_halves[h]], a_listed[:], ACT.Sigmoid, scale=steep_col[:])
        boost_row = sb.tile([P, SLOTS], F32, name="boost_row")
        nc.vector.tensor_copy(boost_row[:].rearrange("p (n j) -> p n j", j=4), boost_ps[:].rearrange("p j n -> p n j"))

        g_bf = sb.tile([P, P, PACK], BF16, name="g_bf", align_bytes=64)
        g_codes = sb.tile([P, P], U32, name="g_codes", align_bytes=64)
        g_scales = sb.tile([P, P], U8, name="g_scales", align_bytes=64)
        v_bf = [sb.tile([P, CHUNK, PACK], BF16, name=f"v_bf{c}", tag=("a_listed1" if c == 0 else f"v_bf{c}"), align_bytes=64) for c in range(len(chunks))]
        v_codes = sb.tile([P, T], U32, name="v_codes", align_bytes=64)
        v_scales = sb.tile([P, T], U8, name="v_scales", align_bytes=64)

        def quantise_vals(c):
            nc.vector.quantize_mx(
                v_codes[:, chunks[c]].bitcast(FP8X4), v_scales[:, chunks[c]], v_bf[c][:].rearrange("p t j -> p (t j)")
            )

        interleave(nc.scalar.copy, g_bf[:], g_raw[:])
        nc.vector.quantize_mx(g_codes[:].bitcast(FP8X4), g_scales[:], g_bf[:].rearrange("p q j -> p (q j)"))
        for c in range(len(chunks)):
            interleave(nc.scalar.copy, v_bf[c][:], v_raw[c][:])

        nc.vector.tensor_tensor(bf[:].indirect(offsets[:]), b_sig[:], boost_row[:], ALU.mult)

        quantise_vals(0)
        quantise_vals(1)
        s = sb.tile([P, T], F32, name="s", tag="v_bf1", align_bytes=64)
        nc.vector.tensor_tensor(s[:], a_sb[:], bf[:], ALU.add)
        quantise_vals(2)
        neg_max = sb.tile([P, 1], F32, name="neg_max")
        nc.vector.tensor_reduce(neg_max[:], s[:], mybir.AxisListType.X, ALU.max, negate=True)
        quantise_vals(3)

        c0_ps = [ps.tile([P, BANK], F32, name=f"c0_ps{h}", tag=f"c0_ps{h}") for h in range(2)]
        for h in range(2):
            nc.tensor.matmul_mx(
                c0_ps[h][:],
                lhsT=g_codes[:].bitcast(FP8X4),
                lhsT_scale=g_scales[:],
                rhs=v_codes[:, halves[h]].bitcast(FP8X4),
                rhs_scale=v_scales[:, halves[h]],
                start=True,
                stop=True,
            )

        p = sb.tile([P, T], F32, name="p")
        z = sb.tile([P, 1], F32, name="z")
        nc.scalar.activation(p[:], s[:], ACT.Exp, bias=neg_max[:], accum_out=z[:])
        neg_u = sb.tile([P, T], F32, name="neg_u")
        for h in range(2):
            nc.vector.scalar_tensor_tensor(
                neg_u[:, halves[h]], c0_ps[h][:], -1.0, fac_row[:, halves[h]], ALU.mult, ALU.mult
            )
        inv_z = sb.tile([P, 1], F32, name="inv_z", tag="inv_z")
        nc.vector.reciprocal(inv_z[:], z[:])
        pn = sb.tile([P, T], F32, name="pn")
        nc.scalar.activation(pn[:], p[:], ACT.Copy, scale=inv_z[:])
        neg_w = sb.tile([P, T], F32, name="neg_w")
        neg_c = sb.tile([P, 1], F32, name="neg_c")
        nc.vector.scalar_tensor_tensor(neg_w[:], neg_u[:], inv_z[:], p[:], ALU.mult, ALU.mult, accum_out=neg_c[:])
        b_sq = sb.tile([P, SLOTS], F32, name="b_sq", tag="inv_z")
        nc.scalar.activation(b_sq[:], b_sig[:], ACT.Square, bias=neg_half[:])
        slope = sb.tile([P, SLOTS], F32, name="slope")
        nc.scalar.activation(slope[:], b_sq[:], ACT.Identity, bias=quarter_steep[:], scale=neg_steep[:])
        old_t = sb.tile([P, T], F32, name="old_t", tag="inv_z")
        base_ps = [ps.tile([P, BANK], F32, name=f"base_ps{h}") for h in range(2)]
        for h in range(2):
            old_ps = ps.tile([P, 4, P], F32, name=f"old_ps{h}", tag=f"c0_ps{h}")
            for j in range(4):
                nc.tensor.transpose(old_ps[:, j, :], old_sb[:, blocks[4 * h + j]], ident[:])
            nc.scalar.copy(old_t[:, halves[h]], old_ps[:].rearrange("p j n -> p (j n)"))
        for h in range(2):
            for j in range(4):
                nc.tensor.matmul(
                    base_ps[h][:, blocks[j]], old_t[:, blocks[4 * h + j]], ident[:], start=(j == 0), stop=False, is_transpose=True
                )
        ds = sb.tile([P, T], F32, name="ds")
        nc.vector.scalar_tensor_tensor(ds[:], pn[:], neg_c[:], neg_w[:], ALU.mult, ALU.subtract)

        db = sb.tile([P, SLOTS], F32, name="db")
        nc.vector.tensor_tensor(db[:], ds[:].indirect(offsets[:]), boost_row[:], ALU.mult)
        ds_t = sb.tile([P, T], F32, name="ds_t")
        for h in range(2):
            ds_ps = ps.tile([P, BANK], F32, name=f"ds_ps{h}", tag=f"a_ps{h}")
            for j in range(4):
                nc.tensor.transpose(ds_ps[:, blocks[j]], ds[:, blocks[4 * h + j]], ident[:])
            nc.scalar.activation(ds_t[:, halves[h]], ds_ps[:], ACT.Copy, scale=OUT_SCALE)
        for h in range(2):
            for j in range(4):
                nc.tensor.matmul(
                    base_ps[h][:, blocks[j]], ds_t[:, blocks[4 * h + j]], ident[:], start=False, stop=(j == 3), is_transpose=True
                )
        nc.vector.tensor_tensor(s1[:].indirect(offsets[:]), db[:], slope[:], ALU.mult)

        for c in range(len(chunks)):
            res = sb.tile([P, CHUNK], F32, name=f"res{c}")
            nc.vector.scalar_tensor_tensor(
                res[:], s1[:, chunks[c]], OUT_SCALE, base_ps[c // 2][:, chunks[c % 2]], ALU.mult, ALU.add
            )
            nc.sync.dma_start(out[:, chunks[c]], res[:])
